import numpy as np
import ml_dtypes


def mxq(x, axis, fmt="e4m3"):
    dtype, down = {"e4m3": (ml_dtypes.float8_e4m3fn, 7), "e5m2": (ml_dtypes.float8_e5m2, 14)}[fmt]
    v = np.moveaxis(np.asarray(x, np.float32).astype(ml_dtypes.bfloat16).astype(np.float64), axis, -1)
    blocks = v.reshape(v.shape[:-1] + (-1, 32))
    amax = np.abs(blocks).max(-1, keepdims=True)
    byte = np.maximum(np.where(amax > 0, np.frexp(amax)[1] - 1 + 127, 0) - down, 1)
    scale = np.exp2(byte - 127.0)
    codes = (blocks / scale).astype(np.float32).astype(dtype).astype(np.float64)
    return np.moveaxis((codes * scale).reshape(v.shape), -1, axis)


WIDE = False


def mx_kscale(k):
    if not WIDE:
        return np.ones(k)
    levels = np.array([10, -10, 5, -5, 0])
    if k % 512:
        return np.exp2(np.random.permutation(np.resize(levels, k // 32))).repeat(32)
    a = np.empty((k // 512, 16))
    for p in range(k // 512):
        a[p, :8] = np.random.permutation(np.resize(levels, 8))
        for g in range(8):
            far = levels[np.abs(levels - a[p, g]) >= 10]
            a[p, g + 8] = far[np.random.randint(len(far))]
    return np.exp2(a.ravel()).repeat(32)


def f64(x):
    return np.asarray(x).astype(np.float64)


def striped(idx):
    return np.tile(idx.reshape(-1, 16).T, (8, 1)).astype(np.uint16)


def unstriped(offs):
    return offs[:16].T.reshape(-1).astype(np.int64)


def striped8(idx):
    return np.concatenate([x.reshape(-1, 16).T for x in idx]).astype(np.uint16)


def runs(offs, k):
    lists = np.stack([offs[16 * r : 16 * r + 16].T.reshape(-1) for r in range(8)]).astype(np.int64)
    return lists[np.arange(k) % 512 // 64]


def pack_weight(w):
    k, n = w.shape
    w = f64(np.asarray(w, np.float32).astype(ml_dtypes.bfloat16)).reshape(k // 32, 32, n)
    amax = np.abs(w).max(1)
    byte = np.clip(np.where(amax > 0, np.frexp(amax)[1] - 1 + 127 - 7, 1), 1, 254)
    scaled = (w * np.exp2(127.0 - byte)[:, None, :]).reshape(k, n).astype(np.float32)
    words = np.ascontiguousarray(scaled.reshape(k // 512, 128, 4, n).transpose(0, 1, 3, 2)).astype(ml_dtypes.float8_e4m3fn).view(np.uint8)
    return words, np.ascontiguousarray(byte.astype(np.uint8).reshape(k // 512, 16, n))


def unpack_weight(words, scales):
    g, p, n, _ = words.shape
    vals = np.ascontiguousarray(words).view(ml_dtypes.float8_e4m3fn).astype(np.float64) * np.repeat(np.exp2(scales.astype(np.float64) - 127.0), 8, axis=1)[..., None]
    return vals.transpose(0, 1, 3, 2).reshape(g * 512, n)


def sigmoid(v):
    return 1.0 / (1.0 + np.exp(-np.maximum(v, -700.0)))


K, T, S, H, W, C, G = 512, 1024, 512, 512, 384, 512, 2048


def setup_inputs():
    n = np.random.standard_normal
    s = mx_kscale(K)[:, None]
    packed_xT = pack_weight(n((K, T)) * s)
    packed_dT = pack_weight(n((K, G)) / s)
    return {
        "x_words": packed_xT[0],
        "x_scales": packed_xT[1],
        "w1": (n((K, H)) / np.sqrt(K) / s).astype(np.float32),
        "gs": (np.random.uniform(0.5, 1.5, (K, 1)) / s).astype(np.float32),
        "gk": (np.random.uniform(0.5, 1.5, (K, 1)) * s).astype(np.float32),
        "d_words": packed_dT[0],
        "d_scales": packed_dT[1],
        "offs": striped(np.random.permutation(T)[:S]),
        "n1": striped(np.random.permutation(S)[:W]),
        "n2": striped(np.random.permutation(S)[:W]),
        "n3": striped(np.random.permutation(S)),
        "n4": striped(np.random.permutation(S)),
        "cand": striped(np.random.permutation(T)[:C]),
        "k1": striped8(np.random.randint(0, G, (8, H))),
        "n5": striped8(np.stack([np.random.permutation(S) for _ in range(8)])),
        "n6": striped8(np.stack([np.random.permutation(S) for _ in range(8)])),
    }


def reference(x_words, x_scales, w1, gs, gk, d_words, d_scales, offs, n1, n2, n3, n4, cand, k1, n5, n6):
    x_cand = unpack_weight(x_words, x_scales)[:, unstriped(cand)]
    xq = unpack_weight(x_words, x_scales)[:, unstriped(offs)]
    y = mxq(f64(w1), 0, "e4m3").T @ xq
    pa = y[:, unstriped(n2)]
    old = y[:, unstriped(n1)]
    ra = np.minimum(pa, old) - (0.5 * pa)
    ds = y.copy()
    ds[:, unstriped(n1)] = ra
    z = f64(gs) * ds
    a = 0.0625 * ((x_cand.T @ mxq(z, 0, "e4m3")))
    d_k1 = unpack_weight(d_words, d_scales)[np.arange(K)[:, None], runs(k1, K)]
    z2 = f64(gk) * (y[:, unstriped(n3)] - y[:, unstriped(n4)])
    b = 0.0625 * ((d_k1.T @ mxq(z2, 0, "e4m3")))
    return (a + a[np.arange(C)[:, None], runs(n5, C)]) * (sigmoid(b + b[np.arange(H)[:, None], runs(n6, H)]))

@@ -1,0 +1,173 @@
+from contextlib import ExitStack
+
+import concourse.mybir as mybir
+
+F32 = mybir.dt.float32
+BF16 = mybir.dt.bfloat16
+U32 = mybir.dt.uint32
+I32 = mybir.dt.int32
+U16 = mybir.dt.uint16
+U8 = mybir.dt.uint8
+FP8X4 = mybir.dt.float8_e4m3fn_x4
+ACT = mybir.ActivationFunctionType
+ALU = mybir.AluOpType
+
+P = 128
+PACK = 4
+T, S, W, G = 1024, 512, 384, 2048
+WIN = 1024
+FLOPS = 3 * 2 * 512 * 512 * 512
+
+
+def tile_picked_cdkeytriebkmingap_none_p_kernel(tc, x_words, x_scales, w1, gs, gk, d_words, d_scales, offs, n1, n2, n3, n4, cand, k1, n5, n6, out):
+    nc = tc.nc
+    with ExitStack() as ctx:
+        keep = ctx.enter_context(tc.tile_pool(name="keep", bufs=1))
+        psum = ctx.enter_context(tc.psum_pool(name="psum", bufs=1))
+
+        def load_list(src, name):
+            tile = keep.tile(list(src.shape), U16, name=name)
+            nc.sync.dma_start(tile[:], src)
+            return tile
+
+        xs = keep.tile([P, T], U8, name="xs", align_bytes=64)
+        nc.vector.memset(xs[:].bitcast(I32), 0)
+        dsc = keep.tile([P, G], U8, name="dsc", align_bytes=64)
+        nc.gpsimd.memset(dsc[:].bitcast(I32), 0)
+        key_scales = keep.tile([P, S], U8, name="key_scales", align_bytes=64)
+        nc.gpsimd.memset(key_scales[:].bitcast(I32), 0)
+
+        for r in range(4):
+            nc.sync.dma_start(xs[r:P:32, :].bitcast(I32), x_scales[0, r:16:4, :].bitcast(I32))
+        l_offs = load_list(offs, "l_offs")
+        xw = keep.tile([P, T], U32, name="xw", align_bytes=64)
+        nc.sync.dma_start(xw[:].bitcast(I32), x_words[0].rearrange("p c r -> p (c r)").bitcast(I32))
+        w_rows = w1.rearrange("(p j) c -> p j c", j=PACK)
+        w_raw = []
+        for h in range(2):
+            raw = keep.tile([P, PACK, 256], F32, name=f"w_raw{h}")
+            nc.sync.dma_start(raw[:], w_rows[:, :, 256 * h : 256 * (h + 1)])
+            w_raw.append(raw)
+        l_n2 = load_list(n2, "l_n2")
+        l_n1 = load_list(n1, "l_n1")
+        gk_t = keep.tile([P, PACK], F32, name="gk_t")
+        nc.sync.dma_start(gk_t[:], gk.rearrange("(p t) o -> p (t o)", t=PACK))
+        l_n4 = load_list(n4, "l_n4")
+        l_n3 = load_list(n3, "l_n3")
+        l_k1 = load_list(k1, "l_k1")
+        nc.sync.dma_start(dsc[0:P:8, :].bitcast(I32), d_scales[0].bitcast(I32))
+        dw = keep.tile([P, G], U32, name="dw", align_bytes=64)
+        nc.sync.dma_start(dw[:].bitcast(I32), d_words[0].rearrange("p c r -> p (c r)").bitcast(I32))
+        l_cand = load_list(cand, "l_cand")
+        gs_t = keep.tile([P, PACK], F32, name="gs_t")
+        nc.sync.dma_start(gs_t[:], gs.rearrange("(p t) o -> p (t o)", t=PACK))
+        l_n6 = load_list(n6, "l_n6")
+        l_n5 = load_list(n5, "l_n5")
+
+        xq_s = keep.tile([P, S], U8, name="xq_s", align_bytes=64)
+        nc.vector.tensor_copy(xq_s[:], xs[:].indirect(l_offs[:]))
+        xq_w = keep.tile([P, S], U32, name="xq_w", align_bytes=64)
+        nc.vector.tensor_copy(xq_w[:], xw[:].indirect(l_offs[:]))
+
+        w_bf = keep.tile([P, PACK, P, PACK], BF16, name="w_bf", align_bytes=64)
+
+        def deal_w(copy, h, m0, m1):
+            copy(w_bf[:, :, 64 * h + m0 : 64 * h + m1, :].rearrange("p t m j -> p m t j"), w_raw[h][:].rearrange("p j (m t) -> p m t j", t=PACK)[:, m0:m1])
+
+        deal_w(nc.scalar.copy, 0, 0, 64)
+        deal_w(nc.vector.tensor_copy, 1, 0, 40)
+        deal_w(nc.scalar.copy, 1, 40, 64)
+        w_q = keep.tile([P, S], U32, name="w_q", align_bytes=64)
+        w_s = keep.tile([P, S], U8, name="w_s", align_bytes=64)
+        nc.vector.quantize_mx(out=w_q[:].bitcast(FP8X4), scales=w_s[:], in_=w_bf[:].rearrange("p t m j -> p (t m j)"))
+
+        def product(tag, t, lw, ls, rw, rs):
+            bank = psum.tile([P, S], F32, name=f"{tag}{t}", tag=f"bank{t + (4 if tag == 'b' else 0)}")
+            cols = slice(P * t, P * (t + 1))
+            nc.tensor.matmul_mx(out=bank[:], lhsT=lw[:, cols].bitcast(FP8X4), lhsT_scale=ls[:, cols], rhs=rw[:].bitcast(FP8X4), rhs_scale=rs[:], start=True, stop=True)
+            return bank
+
+        y, yk, ra = [], [], []
+        for t in range(PACK):
+            bank = product("y", t, w_q, w_s, xq_w, xq_s)
+            y_t = keep.tile([P, WIN], F32, name=f"y{t}")
+            nc.scalar.copy(y_t[:, 0:S], bank[:])
+            half = keep.tile([P, W], F32, name=f"half{t}")
+            nc.scalar.activation(half[:], y_t[:].indirect(l_n2[:]), ACT.Copy, scale=0.5)
+            yk_t = keep.tile([P, WIN], F32, name=f"yk{t}")
+            nc.vector.tensor_scalar(yk_t[:, 0:S], y_t[:, 0:S], gk_t[:, t : t + 1], None, ALU.mult)
+            rest = keep.tile([P, W], F32, name=f"rest{t}")
+            nc.vector.tensor_tensor(rest[:], y_t[:].indirect(l_n1[:]), half[:], ALU.subtract)
+            ra_t = keep.tile([P, W], F32, name=f"ra{t}")
+            nc.vector.tensor_tensor(ra_t[:], rest[:], half[:], ALU.min)
+            y.append(y_t)
+            yk.append(yk_t)
+            ra.append(ra_t)
+
+        z2 = keep.tile([P, PACK, S], F32, name="z2")
+        for t in range(PACK):
+            g4 = keep.tile([P, S], F32, name=f"g4_{t}")
+            nc.scalar.activation(g4[:], yk[t][:].indirect(l_n4[:]), ACT.Copy)
+            nc.vector.tensor_tensor(z2[:, t, :], yk[t][:].indirect(l_n3[:]), g4[:], ALU.subtract)
+
+        dealt = "p (t a b) -> p a t b"
+        dk_s = keep.tile([P, S], U8, name="dk_s", align_bytes=64)
+        nc.vector.tensor_copy(dk_s[:], dsc[:].indirect(l_k1[:]))
+        dk_s2 = keep.tile([P, S], U8, name="dk_s2", align_bytes=64)
+        nc.vector.tensor_copy(dk_s2[:].bitcast(I32).rearrange("p (t a) -> p t a", t=PACK), dk_s[:].bitcast(I32).rearrange("p (a t) -> p t a", t=PACK))
+        for r in range(4):
+            nc.sync.dma_start(key_scales[r:P:32, :].bitcast(I32), dk_s2[8 * r : P : 32, :].bitcast(I32))
+        dk_w = keep.tile([P, S], U32, name="dk_w", align_bytes=64)
+        nc.vector.tensor_copy(dk_w[:], dw[:].indirect(l_k1[:]))
+        key_w = keep.tile([P, S], U32, name="key_w", align_bytes=64)
+        nc.vector.tensor_copy(key_w[:].bitcast(I32).rearrange("p (t a b) -> p t a b", t=PACK, b=4), dk_w[:].bitcast(I32).rearrange("p (a t b) -> p t a b", t=PACK, b=4))
+
+        def quantise(name, planes):
+            woven = keep.tile([P, S, PACK], BF16, name=f"{name}_bf", align_bytes=64)
+            nc.vector.tensor_copy(woven[:].rearrange("p (c i) t -> p c t i", i=4), planes[:].rearrange("p t (c i) -> p c t i", i=4))
+            q = keep.tile([P, S], U32, name=f"{name}_q", align_bytes=64)
+            s = keep.tile([P, S], U8, name=f"{name}_s", align_bytes=64)
+            nc.vector.quantize_mx(out=q[:].bitcast(FP8X4), scales=s[:], in_=woven[:].rearrange("p c t -> p (c t)"))
+            return q, s
+
+        z2_q, z2_s = quantise("z2", z2)
+
+        zb = keep.tile([P, PACK, S], BF16, name="zb")
+        for t in range(PACK):
+            nc.scalar.activation(y[t][:].indirect(l_n1[:]), ra[t][:], ACT.Copy)
+            nc.vector.tensor_scalar(zb[:, t, :], y[t][:, 0:S], gs_t[:, t : t + 1], None, ALU.mult)
+
+        gate = []
+        for t in range(PACK):
+            bank = product("b", t, key_w, key_scales, z2_q, z2_s)
+            b_t = keep.tile([P, WIN], F32, name=f"bw{t}")
+            nc.scalar.activation(b_t[:, 0:S], bank[:], ACT.Copy, scale=0.0625)
+            b_p = keep.tile([P, S], F32, name=f"bp{t}")
+            nc.sync.dma_start(b_p[:], b_t[:, 0:S])
+            u = keep.tile([P, S], F32, name=f"u{t}")
+            nc.vector.tensor_tensor(u[:], b_t[:].indirect(l_n6[:]), b_p[:], ALU.add)
+            g = keep.tile([P, S], F32, name=f"gate{t}")
+            nc.scalar.activation(g[:], u[:], ACT.Tanh, scale=0.5)
+            gate.append(g)
+
+        xc_w = keep.tile([P, S], U32, name="xc_w", align_bytes=64)
+        nc.vector.tensor_copy(xc_w[:].rearrange(dealt, t=PACK, b=4), xw[:].indirect(l_cand[:]))
+        xc_s = keep.tile([P, S], U8, name="xc_s", align_bytes=64)
+        nc.vector.tensor_copy(xc_s[:].rearrange(dealt, t=PACK, b=4), xs[:].indirect(l_cand[:]))
+
+        z_q, z_s = quantise("z", zb)
+        out_rows = out.rearrange("(a t b) c -> t a b c", t=PACK, b=4)
+        for t in range(PACK):
+            bank = product("a", t, xc_w, xc_s, z_q, z_s)
+            a_t = keep.tile([P, WIN], F32, name=f"aw{t}")
+            nc.scalar.activation(a_t[:, 0:S], bank[:], ACT.Copy, scale=0.03125)
+            a5 = keep.tile([P, S], F32, name=f"a5_{t}")
+            if t < 3:
+                nc.scalar.activation(a5[:], a_t[:].indirect(l_n5[:]), ACT.Copy)
+            else:
+                nc.vector.tensor_copy(a5[:], a_t[:].indirect(l_n5[:]))
+            v = keep.tile([P, S], F32, name=f"v{t}")
+            nc.vector.tensor_tensor(v[:], a5[:], a_t[:, 0:S], ALU.add)
+            res = keep.tile([P, S], F32, name=f"res{t}")
+            nc.vector.scalar_tensor_tensor(res[:], gate[t][:], 1.0, v[:], ALU.add, ALU.mult)
+            nc.sync.dma_start(out_rows[t], res[:])

@@ -40,12 +40,13 @@ def tile_picked_cdkeytriebkmingap_none_p_kernel(tc, x_words, x_scales, w1, gs, g
         for r in range(4):
             nc.sync.dma_start(xs[r:P:32, :].bitcast(I32), x_scales[0, r:16:4, :].bitcast(I32))
         l_offs = load_list(offs, "l_offs")
+        l_cand = load_list(cand, "l_cand")
         xw = keep.tile([P, T], U32, name="xw", align_bytes=64)
         nc.sync.dma_start(xw[:].bitcast(I32), x_words[0].rearrange("p c r -> p (c r)").bitcast(I32))
         w_rows = w1.rearrange("(p j) c -> p j c", j=PACK)
         w_raw = []
         for h in range(2):
-            raw = keep.tile([P, PACK, 256], F32, name=f"w_raw{h}")
+            raw = keep.tile([P, PACK, 256], F32, name=f"w_raw{h}", align_bytes=64)
             nc.sync.dma_start(raw[:], w_rows[:, :, 256 * h : 256 * (h + 1)])
             w_raw.append(raw)
         l_n2 = load_list(n2, "l_n2")
@@ -54,11 +55,10 @@ def tile_picked_cdkeytriebkmingap_none_p_kernel(tc, x_words, x_scales, w1, gs, g
         nc.sync.dma_start(gk_t[:], gk.rearrange("(p t) o -> p (t o)", t=PACK))
         l_n4 = load_list(n4, "l_n4")
         l_n3 = load_list(n3, "l_n3")
-        l_k1 = load_list(k1, "l_k1")
-        nc.sync.dma_start(dsc[0:P:8, :].bitcast(I32), d_scales[0].bitcast(I32))
         dw = keep.tile([P, G], U32, name="dw", align_bytes=64)
         nc.sync.dma_start(dw[:].bitcast(I32), d_words[0].rearrange("p c r -> p (c r)").bitcast(I32))
-        l_cand = load_list(cand, "l_cand")
+        l_k1 = load_list(k1, "l_k1")
+        nc.sync.dma_start(dsc[0:P:8, :].bitcast(I32), d_scales[0].bitcast(I32))
         gs_t = keep.tile([P, PACK], F32, name="gs_t")
         nc.sync.dma_start(gs_t[:], gs.rearrange("(p t) o -> p (t o)", t=PACK))
         l_n6 = load_list(n6, "l_n6")
@@ -75,8 +75,8 @@ def tile_picked_cdkeytriebkmingap_none_p_kernel(tc, x_words, x_scales, w1, gs, g
             copy(w_bf[:, :, 64 * h + m0 : 64 * h + m1, :].rearrange("p t m j -> p m t j"), w_raw[h][:].rearrange("p j (m t) -> p m t j", t=PACK)[:, m0:m1])
 
         deal_w(nc.scalar.copy, 0, 0, 64)
-        deal_w(nc.vector.tensor_copy, 1, 0, 40)
-        deal_w(nc.scalar.copy, 1, 40, 64)
+        deal_w(nc.vector.tensor_copy, 1, 0, 36)
+        deal_w(nc.scalar.copy, 1, 36, 64)
         w_q = keep.tile([P, S], U32, name="w_q", align_bytes=64)
         w_s = keep.tile([P, S], U8, name="w_s", align_bytes=64)
         nc.vector.quantize_mx(out=w_q[:].bitcast(FP8X4), scales=w_s[:], in_=w_bf[:].rearrange("p t m j -> p (t m j)"))
@@ -87,38 +87,55 @@ def tile_picked_cdkeytriebkmingap_none_p_kernel(tc, x_words, x_scales, w1, gs, g
             nc.tensor.matmul_mx(out=bank[:], lhsT=lw[:, cols].bitcast(FP8X4), lhsT_scale=ls[:, cols], rhs=rw[:].bitcast(FP8X4), rhs_scale=rs[:], start=True, stop=True)
             return bank
 
-        y, yk, ra = [], [], []
-        for t in range(PACK):
-            bank = product("y", t, w_q, w_s, xq_w, xq_s)
-            y_t = keep.tile([P, WIN], F32, name=f"y{t}")
-            nc.scalar.copy(y_t[:, 0:S], bank[:])
-            half = keep.tile([P, W], F32, name=f"half{t}")
-            nc.scalar.activation(half[:], y_t[:].indirect(l_n2[:]), ACT.Copy, scale=0.5)
-            yk_t = keep.tile([P, WIN], F32, name=f"yk{t}")
-            nc.vector.tensor_scalar(yk_t[:, 0:S], y_t[:, 0:S], gk_t[:, t : t + 1], None, ALU.mult)
-            rest = keep.tile([P, W], F32, name=f"rest{t}")
-            nc.vector.tensor_tensor(rest[:], y_t[:].indirect(l_n1[:]), half[:], ALU.subtract)
-            ra_t = keep.tile([P, W], F32, name=f"ra{t}")
-            nc.vector.tensor_tensor(ra_t[:], rest[:], half[:], ALU.min)
-            y.append(y_t)
-            yk.append(yk_t)
-            ra.append(ra_t)
+        def pipeline(*stages):
+            for step in range(PACK + len(stages) - 1):
+                for k, stage in enumerate(stages):
+                    if 0 <= step - k < PACK:
+                        stage(step - k)
+
+        def tiles(name, width, dtype=F32):
+            return [keep.tile([P, width], dtype, name=f"{name}{t}") for t in range(PACK)]
+
+        y, yk, half, rest, ra = tiles("y", WIN), tiles("yk", WIN), tiles("half", W), tiles("rest", W), tiles("ra", W)
+
+        def project(t):
+            nc.scalar.copy(y[t][:, 0:S], product("y", t, w_q, w_s, xq_w, xq_s)[:])
+
+        def fetch_half(t):
+            nc.scalar.activation(half[t][:], y[t][:].indirect(l_n2[:]), ACT.Copy, scale=0.5)
+            nc.vector.tensor_scalar(yk[t][:, 0:S], y[t][:, 0:S], gk_t[:, t : t + 1], None, ALU.mult)
+
+        def fetch_rest(t):
+            nc.vector.tensor_tensor(rest[t][:], y[t][:].indirect(l_n1[:]), half[t][:], ALU.subtract)
+
+        def smaller(t):
+            nc.vector.tensor_tensor(ra[t][:], rest[t][:], half[t][:], ALU.min)
+
+        pipeline(project, fetch_half, fetch_rest, smaller)
 
         z2 = keep.tile([P, PACK, S], F32, name="z2")
-        for t in range(PACK):
-            g4 = keep.tile([P, S], F32, name=f"g4_{t}")
-            nc.scalar.activation(g4[:], yk[t][:].indirect(l_n4[:]), ACT.Copy)
-            nc.vector.tensor_tensor(z2[:, t, :], yk[t][:].indirect(l_n3[:]), g4[:], ALU.subtract)
+        g4 = tiles("g4_", S)
+
+        def fetch_n4(t):
+            if t < 3:
+                nc.scalar.activation(g4[t][:], yk[t][:].indirect(l_n4[:]), ACT.Copy)
+            else:
+                nc.vector.tensor_copy(g4[t][:], yk[t][:].indirect(l_n4[:]))
+
+        def fetch_n3(t):
+            nc.vector.tensor_tensor(z2[:, t, :], yk[t][:].indirect(l_n3[:]), g4[t][:], ALU.subtract)
+
+        pipeline(fetch_n4, fetch_n3)
 
         dealt = "p (t a b) -> p a t b"
         dk_s = keep.tile([P, S], U8, name="dk_s", align_bytes=64)
         nc.vector.tensor_copy(dk_s[:], dsc[:].indirect(l_k1[:]))
+        dk_w = keep.tile([P, S], U32, name="dk_w", align_bytes=64)
+        nc.vector.tensor_copy(dk_w[:], dw[:].indirect(l_k1[:]))
         dk_s2 = keep.tile([P, S], U8, name="dk_s2", align_bytes=64)
         nc.vector.tensor_copy(dk_s2[:].bitcast(I32).rearrange("p (t a) -> p t a", t=PACK), dk_s[:].bitcast(I32).rearrange("p (a t) -> p t a", t=PACK))
         for r in range(4):
             nc.sync.dma_start(key_scales[r:P:32, :].bitcast(I32), dk_s2[8 * r : P : 32, :].bitcast(I32))
-        dk_w = keep.tile([P, S], U32, name="dk_w", align_bytes=64)
-        nc.vector.tensor_copy(dk_w[:], dw[:].indirect(l_k1[:]))
         key_w = keep.tile([P, S], U32, name="key_w", align_bytes=64)
         nc.vector.tensor_copy(key_w[:].bitcast(I32).rearrange("p (t a b) -> p t a b", t=PACK, b=4), dk_w[:].bitcast(I32).rearrange("p (a t b) -> p t a b", t=PACK, b=4))
 
@@ -137,37 +154,40 @@ def tile_picked_cdkeytriebkmingap_none_p_kernel(tc, x_words, x_scales, w1, gs, g
             nc.scalar.activation(y[t][:].indirect(l_n1[:]), ra[t][:], ACT.Copy)
             nc.vector.tensor_scalar(zb[:, t, :], y[t][:, 0:S], gs_t[:, t : t + 1], None, ALU.mult)
 
-        gate = []
-        for t in range(PACK):
-            bank = product("b", t, key_w, key_scales, z2_q, z2_s)
-            b_t = keep.tile([P, WIN], F32, name=f"bw{t}")
-            nc.scalar.activation(b_t[:, 0:S], bank[:], ACT.Copy, scale=0.0625)
-            b_p = keep.tile([P, S], F32, name=f"bp{t}")
-            nc.sync.dma_start(b_p[:], b_t[:, 0:S])
-            u = keep.tile([P, S], F32, name=f"u{t}")
-            nc.vector.tensor_tensor(u[:], b_t[:].indirect(l_n6[:]), b_p[:], ALU.add)
-            g = keep.tile([P, S], F32, name=f"gate{t}")
-            nc.scalar.activation(g[:], u[:], ACT.Tanh, scale=0.5)
-            gate.append(g)
-
-        xc_w = keep.tile([P, S], U32, name="xc_w", align_bytes=64)
+        xc_w = keep.tile([P, S], U32, name="xc_w", tag="w_raw1", align_bytes=64)
         nc.vector.tensor_copy(xc_w[:].rearrange(dealt, t=PACK, b=4), xw[:].indirect(l_cand[:]))
         xc_s = keep.tile([P, S], U8, name="xc_s", align_bytes=64)
         nc.vector.tensor_copy(xc_s[:].rearrange(dealt, t=PACK, b=4), xs[:].indirect(l_cand[:]))
 
-        z_q, z_s = quantise("z", zb)
         out_rows = out.rearrange("(a t b) c -> t a b c", t=PACK, b=4)
+        bw, b_other, u, gate = tiles("bw", WIN), tiles("b_other", S), tiles("u", S), tiles("gate", S)
+        aw, a_other, v, res = tiles("aw", WIN), tiles("a_other", S), tiles("v", S), tiles("res", S)
+        A_FUSED = 1
+
         for t in range(PACK):
-            bank = product("a", t, xc_w, xc_s, z_q, z_s)
-            a_t = keep.tile([P, WIN], F32, name=f"aw{t}")
-            nc.scalar.activation(a_t[:, 0:S], bank[:], ACT.Copy, scale=0.03125)
-            a5 = keep.tile([P, S], F32, name=f"a5_{t}")
-            if t < 3:
-                nc.scalar.activation(a5[:], a_t[:].indirect(l_n5[:]), ACT.Copy)
+            nc.scalar.activation(bw[t][:, 0:S], product("b", t, key_w, key_scales, z2_q, z2_s)[:], ACT.Copy, scale=0.0625)
+            nc.sync.dma_start(b_other[t][:], bw[t][:, 0:S])
+        z_q, z_s = quantise("z", zb)
+        for t in range(PACK):
+            nc.scalar.activation(aw[t][:, 0:S], product("a", t, xc_w, xc_s, z_q, z_s)[:], ACT.Copy, scale=0.03125)
+            if t < A_FUSED:
+                nc.sync.dma_start(a_other[t][:], aw[t][:, 0:S])
+        for t in range(PACK):
+            nc.vector.tensor_tensor(u[t][:], bw[t][:].indirect(l_n6[:]), b_other[t][:], ALU.add)
+
+        def fetch_n5(t):
+            if t >= A_FUSED:
+                nc.scalar.activation(a_other[t][:], aw[t][:].indirect(l_n5[:]), ACT.Copy)
+            nc.scalar.activation(gate[t][:], u[t][:], ACT.Tanh, scale=0.5)
+
+        def sums(t):
+            if t < A_FUSED:
+                nc.vector.tensor_tensor(v[t][:], aw[t][:].indirect(l_n5[:]), a_other[t][:], ALU.add)
             else:
-                nc.vector.tensor_copy(a5[:], a_t[:].indirect(l_n5[:]))
-            v = keep.tile([P, S], F32, name=f"v{t}")
-            nc.vector.tensor_tensor(v[:], a5[:], a_t[:, 0:S], ALU.add)
-            res = keep.tile([P, S], F32, name=f"res{t}")
-            nc.vector.scalar_tensor_tensor(res[:], gate[t][:], 1.0, v[:], ALU.add, ALU.mult)
-            nc.sync.dma_start(out_rows[t], res[:])
+                nc.vector.tensor_tensor(v[t][:], a_other[t][:], aw[t][:, 0:S], ALU.add)
+
+        def finish(t):
+            nc.vector.scalar_tensor_tensor(res[t][:], gate[t][:], 1.0, v[t][:], ALU.add, ALU.mult)
+            nc.sync.dma_start(out_rows[t], res[t][:])
+
+        pipeline(fetch_n5, sums, finish)

@@ -164,9 +164,13 @@ def tile_picked_cdkeytriebkmingap_none_p_kernel(tc, x_words, x_scales, w1, gs, g
         aw, a_other, v, res = tiles("aw", WIN), tiles("a_other", S), tiles("v", S), tiles("res", S)
         A_FUSED = 1
 
-        for t in range(PACK):
-            nc.scalar.activation(bw[t][:, 0:S], product("b", t, key_w, key_scales, z2_q, z2_s)[:], ACT.Copy, scale=0.0625)
-            nc.sync.dma_start(b_other[t][:], bw[t][:, 0:S])
+        for t in (2, 3, 0, 1):
+            bank = product("b", t, key_w, key_scales, z2_q, z2_s)
+            nc.scalar.activation(bw[t][:, 0:S], bank[:], ACT.Copy, scale=0.0625)
+            if t >= 2:
+                nc.sync.dma_start(b_other[t][:], bw[t][:, 0:S])
+            else:
+                nc.scalar.activation(b_other[t][:], bank[:], ACT.Copy, scale=0.0625)
         z_q, z_s = quantise("z", zb)
         for t in range(PACK):
             nc.scalar.activation(aw[t][:, 0:S], product("a", t, xc_w, xc_s, z_q, z_s)[:], ACT.Copy, scale=0.03125)
@@ -175,19 +179,26 @@ def tile_picked_cdkeytriebkmingap_none_p_kernel(tc, x_words, x_scales, w1, gs, g
         for t in range(PACK):
             nc.vector.tensor_tensor(u[t][:], bw[t][:].indirect(l_n6[:]), b_other[t][:], ALU.add)
 
-        def fetch_n5(t):
-            if t >= A_FUSED:
-                nc.scalar.activation(a_other[t][:], aw[t][:].indirect(l_n5[:]), ACT.Copy)
-            nc.scalar.activation(gate[t][:], u[t][:], ACT.Tanh, scale=0.5)
+        pieces = [(t, 0, S) for t in range(PACK - 1)] + [(PACK - 1, 0, S // 2), (PACK - 1, S // 2, S)]
 
-        def sums(t):
+        def fetch_n5(t, c0, c1):
+            if t >= A_FUSED:
+                nc.scalar.activation(a_other[t][:, c0:c1], aw[t][:].indirect(l_n5[:, c0 // 16 : c1 // 16]), ACT.Copy)
+            if c0 == 0:
+                nc.scalar.activation(gate[t][:], u[t][:], ACT.Tanh, scale=0.5)
+
+        def sums(t, c0, c1):
             if t < A_FUSED:
                 nc.vector.tensor_tensor(v[t][:], aw[t][:].indirect(l_n5[:]), a_other[t][:], ALU.add)
             else:
-                nc.vector.tensor_tensor(v[t][:], a_other[t][:], aw[t][:, 0:S], ALU.add)
+                nc.vector.tensor_tensor(v[t][:, c0:c1], a_other[t][:, c0:c1], aw[t][:, c0:c1], ALU.add)
 
-        def finish(t):
-            nc.vector.scalar_tensor_tensor(res[t][:], gate[t][:], 1.0, v[t][:], ALU.add, ALU.mult)
-            nc.sync.dma_start(out_rows[t], res[t][:])
+        def finish(t, c0, c1):
+            nc.vector.scalar_tensor_tensor(res[t][:, c0:c1], gate[t][:, c0:c1], 1.0, v[t][:, c0:c1], ALU.add, ALU.mult)
+            nc.sync.dma_start(out_rows[t][:, :, c0:c1], res[t][:, c0:c1])
 
-        pipeline(fetch_n5, sums, finish)
+        stages = (fetch_n5, sums, finish)
+        for step in range(len(pieces) + len(stages) - 1):
+            for k, stage in enumerate(stages):
+                if 0 <= step - k < len(pieces):
+                    stage(*pieces[step - k])

from contextlib import ExitStack

import concourse.mybir as mybir

F32 = mybir.dt.float32
BF16 = mybir.dt.bfloat16
U32 = mybir.dt.uint32
I32 = mybir.dt.int32
U16 = mybir.dt.uint16
U8 = mybir.dt.uint8
FP8X4 = mybir.dt.float8_e4m3fn_x4
ACT = mybir.ActivationFunctionType
ALU = mybir.AluOpType

P = 128
PACK = 4
T, S, W, G = 1024, 512, 384, 2048
WIN = 1024
FLOPS = 3 * 2 * 512 * 512 * 512


def tile_picked_cdkeytriebkmingap_none_p_kernel(tc, x_words, x_scales, w1, gs, gk, d_words, d_scales, offs, n1, n2, n3, n4, cand, k1, n5, n6, out):
    nc = tc.nc
    with ExitStack() as ctx:
        keep = ctx.enter_context(tc.tile_pool(name="keep", bufs=1))
        psum = ctx.enter_context(tc.psum_pool(name="psum", bufs=1))

        def load_list(src, name):
            tile = keep.tile(list(src.shape), U16, name=name)
            nc.sync.dma_start(tile[:], src)
            return tile

        xs = keep.tile([P, T], U8, name="xs", align_bytes=64)
        nc.vector.memset(xs[:].bitcast(I32), 0)
        dsc = keep.tile([P, G], U8, name="dsc", align_bytes=64)
        nc.gpsimd.memset(dsc[:].bitcast(I32), 0)
        key_scales = keep.tile([P, S], U8, name="key_scales", align_bytes=64)
        nc.gpsimd.memset(key_scales[:].bitcast(I32), 0)

        for r in range(4):
            nc.sync.dma_start(xs[r:P:32, :].bitcast(I32), x_scales[0, r:16:4, :].bitcast(I32))
        l_offs = load_list(offs, "l_offs")
        l_cand = load_list(cand, "l_cand")
        xw = keep.tile([P, T], U32, name="xw", align_bytes=64)
        nc.sync.dma_start(xw[:].bitcast(I32), x_words[0].rearrange("p c r -> p (c r)").bitcast(I32))
        w_rows = w1.rearrange("(p j) c -> p j c", j=PACK)
        w_raw = []
        for h in range(2):
            raw = keep.tile([P, PACK, 256], F32, name=f"w_raw{h}", align_bytes=64)
            nc.sync.dma_start(raw[:], w_rows[:, :, 256 * h : 256 * (h + 1)])
            w_raw.append(raw)
        l_n2 = load_list(n2, "l_n2")
        l_n1 = load_list(n1, "l_n1")
        gk_t = keep.tile([P, PACK], F32, name="gk_t")
        nc.sync.dma_start(gk_t[:], gk.rearrange("(p t) o -> p (t o)", t=PACK))
        l_n4 = load_list(n4, "l_n4")
        l_n3 = load_list(n3, "l_n3")
        dw = keep.tile([P, G], U32, name="dw", align_bytes=64)
        nc.sync.dma_start(dw[:].bitcast(I32), d_words[0].rearrange("p c r -> p (c r)").bitcast(I32))
        l_k1 = load_list(k1, "l_k1")
        nc.sync.dma_start(dsc[0:P:8, :].bitcast(I32), d_scales[0].bitcast(I32))
        gs_t = keep.tile([P, PACK], F32, name="gs_t")
        nc.sync.dma_start(gs_t[:], gs.rearrange("(p t) o -> p (t o)", t=PACK))
        l_n6 = load_list(n6, "l_n6")
        l_n5 = load_list(n5, "l_n5")

        xq_s = keep.tile([P, S], U8, name="xq_s", align_bytes=64)
        nc.vector.tensor_copy(xq_s[:], xs[:].indirect(l_offs[:]))
        xq_w = keep.tile([P, S], U32, name="xq_w", align_bytes=64)
        nc.vector.tensor_copy(xq_w[:], xw[:].indirect(l_offs[:]))

        w_bf = keep.tile([P, PACK, P, PACK], BF16, name="w_bf", align_bytes=64)

        def deal_w(copy, h, m0, m1):
            copy(w_bf[:, :, 64 * h + m0 : 64 * h + m1, :].rearrange("p t m j -> p m t j"), w_raw[h][:].rearrange("p j (m t) -> p m t j", t=PACK)[:, m0:m1])

        deal_w(nc.scalar.copy, 0, 0, 64)
        deal_w(nc.vector.tensor_copy, 1, 0, 36)
        deal_w(nc.scalar.copy, 1, 36, 64)
        w_q = keep.tile([P, S], U32, name="w_q", align_bytes=64)
        w_s = keep.tile([P, S], U8, name="w_s", align_bytes=64)
        nc.vector.quantize_mx(out=w_q[:].bitcast(FP8X4), scales=w_s[:], in_=w_bf[:].rearrange("p t m j -> p (t m j)"))

        def product(tag, t, lw, ls, rw, rs):
            bank = psum.tile([P, S], F32, name=f"{tag}{t}", tag=f"bank{t + (4 if tag == 'b' else 0)}")
            cols = slice(P * t, P * (t + 1))
            nc.tensor.matmul_mx(out=bank[:], lhsT=lw[:, cols].bitcast(FP8X4), lhsT_scale=ls[:, cols], rhs=rw[:].bitcast(FP8X4), rhs_scale=rs[:], start=True, stop=True)
            return bank

        def pipeline(*stages):
            for step in range(PACK + len(stages) - 1):
                for k, stage in enumerate(stages):
                    if 0 <= step - k < PACK:
                        stage(step - k)

        def tiles(name, width, dtype=F32):
            return [keep.tile([P, width], dtype, name=f"{name}{t}") for t in range(PACK)]

        y, yk, half, rest, ra = tiles("y", WIN), tiles("yk", WIN), tiles("half", W), tiles("rest", W), tiles("ra", W)

        def project(t):
            nc.scalar.copy(y[t][:, 0:S], product("y", t, w_q, w_s, xq_w, xq_s)[:])

        def fetch_half(t):
            nc.scalar.activation(half[t][:], y[t][:].indirect(l_n2[:]), ACT.Copy, scale=0.5)
            nc.vector.tensor_scalar(yk[t][:, 0:S], y[t][:, 0:S], gk_t[:, t : t + 1], None, ALU.mult)

        def fetch_rest(t):
            nc.vector.tensor_tensor(rest[t][:], y[t][:].indirect(l_n1[:]), half[t][:], ALU.subtract)

        def smaller(t):
            nc.vector.tensor_tensor(ra[t][:], rest[t][:], half[t][:], ALU.min)

        pipeline(project, fetch_half, fetch_rest, smaller)

        z2 = keep.tile([P, PACK, S], F32, name="z2")
        g4 = tiles("g4_", S)

        def fetch_n4(t):
            if t < 3:
                nc.scalar.activation(g4[t][:], yk[t][:].indirect(l_n4[:]), ACT.Copy)
            else:
                nc.vector.tensor_copy(g4[t][:], yk[t][:].indirect(l_n4[:]))

        def fetch_n3(t):
            nc.vector.tensor_tensor(z2[:, t, :], yk[t][:].indirect(l_n3[:]), g4[t][:], ALU.subtract)

        pipeline(fetch_n4, fetch_n3)

        dealt = "p (t a b) -> p a t b"
        dk_s = keep.tile([P, S], U8, name="dk_s", align_bytes=64)
        nc.vector.tensor_copy(dk_s[:], dsc[:].indirect(l_k1[:]))
        dk_w = keep.tile([P, S], U32, name="dk_w", align_bytes=64)
        nc.vector.tensor_copy(dk_w[:], dw[:].indirect(l_k1[:]))
        dk_s2 = keep.tile([P, S], U8, name="dk_s2", align_bytes=64)
        nc.vector.tensor_copy(dk_s2[:].bitcast(I32).rearrange("p (t a) -> p t a", t=PACK), dk_s[:].bitcast(I32).rearrange("p (a t) -> p t a", t=PACK))
        for r in range(4):
            nc.sync.dma_start(key_scales[r:P:32, :].bitcast(I32), dk_s2[8 * r : P : 32, :].bitcast(I32))
        key_w = keep.tile([P, S], U32, name="key_w", align_bytes=64)
        nc.vector.tensor_copy(key_w[:].bitcast(I32).rearrange("p (t a b) -> p t a b", t=PACK, b=4), dk_w[:].bitcast(I32).rearrange("p (a t b) -> p t a b", t=PACK, b=4))

        def quantise(name, planes):
            woven = keep.tile([P, S, PACK], BF16, name=f"{name}_bf", align_bytes=64)
            nc.vector.tensor_copy(woven[:].rearrange("p (c i) t -> p c t i", i=4), planes[:].rearrange("p t (c i) -> p c t i", i=4))
            q = keep.tile([P, S], U32, name=f"{name}_q", align_bytes=64)
            s = keep.tile([P, S], U8, name=f"{name}_s", align_bytes=64)
            nc.vector.quantize_mx(out=q[:].bitcast(FP8X4), scales=s[:], in_=woven[:].rearrange("p c t -> p (c t)"))
            return q, s

        z2_q, z2_s = quantise("z2", z2)

        zb = keep.tile([P, PACK, S], BF16, name="zb")
        for t in range(PACK):
            nc.scalar.activation(y[t][:].indirect(l_n1[:]), ra[t][:], ACT.Copy)
            nc.vector.tensor_scalar(zb[:, t, :], y[t][:, 0:S], gs_t[:, t : t + 1], None, ALU.mult)

        xc_w = keep.tile([P, S], U32, name="xc_w", tag="w_raw1", align_bytes=64)
        nc.vector.tensor_copy(xc_w[:].rearrange(dealt, t=PACK, b=4), xw[:].indirect(l_cand[:]))
        xc_s = keep.tile([P, S], U8, name="xc_s", align_bytes=64)
        nc.vector.tensor_copy(xc_s[:].rearrange(dealt, t=PACK, b=4), xs[:].indirect(l_cand[:]))

        out_rows = out.rearrange("(a t b) c -> t a b c", t=PACK, b=4)
        bw, b_other, u, gate = tiles("bw", WIN), tiles("b_other", S), tiles("u", S), tiles("gate", S)
        aw, a_other, v, res = tiles("aw", WIN), tiles("a_other", S), tiles("v", S), tiles("res", S)
        A_FUSED = 1

        for t in (2, 3, 0, 1):
            bank = product("b", t, key_w, key_scales, z2_q, z2_s)
            nc.scalar.activation(bw[t][:, 0:S], bank[:], ACT.Copy, scale=0.0625)
            if t >= 2:
                nc.sync.dma_start(b_other[t][:], bw[t][:, 0:S])
            else:
                nc.scalar.activation(b_other[t][:], bank[:], ACT.Copy, scale=0.0625)
        z_q, z_s = quantise("z", zb)
        for t in range(PACK):
            nc.scalar.activation(aw[t][:, 0:S], product("a", t, xc_w, xc_s, z_q, z_s)[:], ACT.Copy, scale=0.03125)
            if t < A_FUSED:
                nc.sync.dma_start(a_other[t][:], aw[t][:, 0:S])
        for t in range(PACK):
            nc.vector.tensor_tensor(u[t][:], bw[t][:].indirect(l_n6[:]), b_other[t][:], ALU.add)

        pieces = [(t, 0, S) for t in range(PACK - 1)] + [(PACK - 1, 0, S // 2), (PACK - 1, S // 2, S)]

        def fetch_n5(t, c0, c1):
            if t >= A_FUSED:
                nc.scalar.activation(a_other[t][:, c0:c1], aw[t][:].indirect(l_n5[:, c0 // 16 : c1 // 16]), ACT.Copy)
            if c0 == 0:
                nc.scalar.activation(gate[t][:], u[t][:], ACT.Tanh, scale=0.5)

        def sums(t, c0, c1):
            if t < A_FUSED:
                nc.vector.tensor_tensor(v[t][:], aw[t][:].indirect(l_n5[:]), a_other[t][:], ALU.add)
            else:
                nc.vector.tensor_tensor(v[t][:, c0:c1], a_other[t][:, c0:c1], aw[t][:, c0:c1], ALU.add)

        def finish(t, c0, c1):
            nc.vector.scalar_tensor_tensor(res[t][:, c0:c1], gate[t][:, c0:c1], 1.0, v[t][:, c0:c1], ALU.add, ALU.mult)
            nc.sync.dma_start(out_rows[t][:, :, c0:c1], res[t][:, c0:c1])

        stages = (fetch_n5, sums, finish)
        for step in range(len(pieces) + len(stages) - 1):
            for k, stage in enumerate(stages):
                if 0 <= step - k < len(pieces):
                    stage(*pieces[step - k])
